import numpy as np, ml_dtypes
CORES = [17,57,65,89,97,121]
N = 6
DEG, TK, TIMES = 5, 64, 2
MASK = [[4,5,0,1,2],[5,0,1,2,3],[0,1,2,3,4],[1,2,3,4,5],[2,3,4,5,0],[3,4,5,0,1]]
def setup_inputs(rng):
    return {"x": rng.standard_normal((N, 128, TK), dtype=np.float32).astype(ml_dtypes.bfloat16), "w": (rng.standard_normal((N, 128, DEG * 128), dtype=np.float32) / np.float32(np.sqrt(128 * DEG / 2))).astype(ml_dtypes.bfloat16)}
def setup_inputs_big(rng):
    d = setup_inputs(rng)
    for k in ("x",): d[k] = (d[k].astype(np.float32) * 1048576.0).astype(d[k].dtype)
    return d
def setup_inputs_small(rng):
    d = setup_inputs(rng)
    for k in ("x",): d[k] = (d[k].astype(np.float32) * (1 / 1048576.0)).astype(d[k].dtype)
    return d
def setup_inputs_apart(rng):
    d = setup_inputs(rng)
    f = (10.0 ** rng.permutation(np.linspace(-1.5, 1.5, N))).astype(np.float32).reshape(N, 1, 1)
    for k in ("x",): d[k] = (d[k].astype(np.float32) * f).astype(d[k].dtype)
    return d
def reference(x, w):
    X, W = x.astype(np.float64), w.astype(np.float64)
    h = list(X)
    for _ in range(TIMES):
        h = [np.maximum(sum(W[r][:, 128 * i:128 * i + 128].T @ h[j] for i, j in enumerate(MASK[r])), 0.0) for r in range(N)]
    return {"y": np.stack(h).astype(ml_dtypes.bfloat16)}

from concourse.bass import DstId, RemoteDMATransfer
from concourse.mybir import AluOpType

NR, DEG, TK, P = 6, 5, 64, 128

SCRATCH = {
    "ws": ("sbuf", [P, DEG * P], "bfloat16"),
    "xme": ("sbuf", [P, TK], "bfloat16"),
    "xin": ("sbuf", [P, DEG * TK], "bfloat16"),
    "hme": ("sbuf", [P, TK], "bfloat16"),
    "hin": ("sbuf", [P, DEG * TK], "bfloat16"),
    "ys": ("sbuf", [P, TK], "bfloat16"),
    "zero": ("sbuf", [P, TK], "float32"),
    "ps1": ("psum", [P, 512], "float32"),
    "ps2": ("psum", [P, 512], "float32"),
}
SEMAPHORES = (["sx%d" % k for k in range(NR)] + ["sh%d" % k for k in range(NR)]
              + ["sw", "sent", "zs", "mm1", "rl1", "mm2", "rl2", "st"])


def _bits(m):
    return [b for b in range(m.bit_length()) if (m >> b) & 1]


def _mask_of(bits):
    m = 0
    for b in bits:
        m |= 1 << b
    return m


def rank_program(g, core, T, topo):
    cores = list(T.cores)
    tab = T.tables["MASK"]
    n = len(cores)
    sem = T.sem

    twin, relay = {}, {}
    for k, c in enumerate(cores):
        owners = [d for d in range(topo.CHIPS * topo.CORES_PER_CHIP)
                  if topo.chip(d) == topo.chip(c) and topo.die(d) == topo.die(c) and d not in cores
                  and all(topo.may_write(d, t) for t in cores)]
        twin[k], relay[k] = owners[0], owners[1]

    def users(k):
        return [j for j in range(n) if j != k and k in tab[j]]

    def near(k):
        return [j for j in users(k) if topo.may_write(cores[k], cores[j])]

    def far(k):
        return [j for j in users(k) if not topo.may_write(cores[k], cores[j])]

    def slot(j, k):
        i = tab[j].index(k)
        return slice(i * TK, (i + 1) * TK)

    rank = T.rank_of(core)
    as_twin = [k for k in range(n) if twin[k] == core]
    as_relay = [k for k in range(n) if relay[k] == core]
    if rank is None and not as_twin and not as_relay:
        return
    me = rank if rank is not None else (as_twin + as_relay)[0]

    away = [c for c in cores if topo.chip(c) != topo.chip(core)][0]
    home = [c for c in (cores[me], twin[me], relay[me]) if c != core][0]
    out_bits = _bits(topo.mask(core, away))
    in_bits = [b for b in _bits(topo.mask(core, home)) if b not in out_bits]
    E_OUT, E_IN = len(out_bits), len(in_bits)
    m_out, m_in = _mask_of(out_bits), _mask_of(in_bits)

    sent = [0]

    def push(src, targets, s, m, cnt):
        ids = [DstId(rid=topo.addr(d)[0], pnc=topo.addr(d)[1]) for d, _ in targets]
        g.remote_dma_fused([RemoteDMATransfer(dst_ids=ids, dma_engine_mask=m, remote_sem=s, srcs=[src],
                                              dsts=[ap for _, ap in targets], alu_op=0)], local_sem=sem.sent)
        sent[0] += cnt

    if as_relay:
        g.wait_ge(sem["sx%d" % me], E_IN)
        push(T.xme[:], [(cores[j], T.xin[:, slot(j, me)]) for j in far(me)], sem["sx%d" % me], m_out, E_OUT)
        g.wait_ge(sem.sent, sent[0])
        return

    sxme = sem["sx%d" % me]
    if rank is not None:
        g.sync.dma_start(T.xme[:], T.x[:]).then_inc(sxme, 16)
        g.scalar.dma_start(T.ws[:], T.w[:]).then_inc(sem.sw, 16)
        x_here, w_here = 16, 16
    else:
        x_here, w_here = E_IN, E_IN
    g.vector.memset(T.zero[:], 0.0).then_inc(sem.zs, 1)

    g.wait_ge(sxme, x_here)
    if rank is not None:
        push(T.xme[:], [(twin[me], T.xme[:]), (relay[me], T.xme[:])], sxme, m_in, E_IN)
        push(T.xme[:], [(d, T.xin[:, slot(j, me)]) for j in near(me) for d in (twin[j], cores[j])], sxme, m_out, E_OUT)
        g.wait_ge(sem.sw, w_here)
        rid, pid = topo.addr(twin[me])[0], topo.addr(twin[me])[1]
        g.remote_dma(T.ws[:], T.ws[:], sem.sw, sem.sent, pid, rid, m_in)
        sent[0] += E_IN
    else:
        push(T.xme[:], [(twin[j], T.xin[:, slot(j, me)]) for j in far(me)], sxme, m_out, E_OUT)

    srcs = [k for k in tab[me] if k == me] + [k for k in tab[me] if k != me and me in near(k)] \
        + [k for k in tab[me] if k != me and me in far(k)]

    def tile(k):
        i = tab[me].index(k)
        return T.ws[:, i * P:(i + 1) * P]

    g.tensor.wait_ge(sem.sw, w_here)
    for a, k in enumerate(srcs):
        g.tensor.wait_ge(sem["sx%d" % k], x_here if k == me else E_OUT)
        mm = g.tensor.matmul(T.ps1[:, 0:TK], tile(k), T.xme[:] if k == me else T.xin[:, slot(me, k)],
                             a == 0, a == len(srcs) - 1)
    mm.then_inc(sem.mm1, 1)
    g.vector.wait_ge(sem.zs, 1)
    g.vector.wait_ge(sem.mm1, 1)
    g.vector.tensor_tensor(T.hme[:], T.ps1[:, 0:TK], T.zero[:], AluOpType.max).then_inc(sem.rl1, 1)

    g.wait_ge(sem.rl1, 1)
    takers = near(me) if rank is not None else far(me)
    push(T.hme[:], [(cores[j], T.hin[:, slot(j, me)]) for j in takers], sem["sh%d" % me], m_out, E_OUT)

    if rank is not None:
        for a, k in enumerate(srcs):
            if k == me:
                g.tensor.wait_ge(sem.rl1, 1)
            else:
                g.tensor.wait_ge(sem["sh%d" % k], E_OUT)
            mm = g.tensor.matmul(T.ps2[:, 0:TK], tile(k), T.hme[:] if k == me else T.hin[:, slot(me, k)],
                                 a == 0, a == len(srcs) - 1)
        mm.then_inc(sem.mm2, 1)
        g.vector.wait_ge(sem.mm2, 1)
        g.vector.tensor_tensor(T.ys[:], T.ps2[:, 0:TK], T.zero[:], AluOpType.max).then_inc(sem.rl2, 1)
        g.sync.wait_ge(sem.rl2, 1)
        g.sync.dma_start(T.y[:], T.ys[:]).then_inc(sem.st, 16)
        g.sync.wait_ge(sem.st, 16)

    g.wait_ge(sem.sent, sent[0])
